import numpy as np
import ml_dtypes


def mxq(x, axis, fmt="e4m3"):
    dtype, down = {"e4m3": (ml_dtypes.float8_e4m3fn, 7), "e5m2": (ml_dtypes.float8_e5m2, 14)}[fmt]
    v = np.moveaxis(np.asarray(x, np.float32).astype(ml_dtypes.bfloat16).astype(np.float64), axis, -1)
    blocks = v.reshape(v.shape[:-1] + (-1, 32))
    amax = np.abs(blocks).max(-1, keepdims=True)
    byte = np.maximum(np.where(amax > 0, np.frexp(amax)[1] - 1 + 127, 0) - down, 1)
    scale = np.exp2(byte - 127.0)
    codes = (blocks / scale).astype(np.float32).astype(dtype).astype(np.float64)
    return np.moveaxis((codes * scale).reshape(v.shape), -1, axis)


WIDE = False


def mx_kscale(k):
    if not WIDE:
        return np.ones(k)
    levels = np.array([10, -10, 5, -5, 0])
    if k % 512:
        return np.exp2(np.random.permutation(np.resize(levels, k // 32))).repeat(32)
    a = np.empty((k // 512, 16))
    for p in range(k // 512):
        a[p, :8] = np.random.permutation(np.resize(levels, 8))
        for g in range(8):
            far = levels[np.abs(levels - a[p, g]) >= 10]
            a[p, g + 8] = far[np.random.randint(len(far))]
    return np.exp2(a.ravel()).repeat(32)


def f64(x):
    return np.asarray(x).astype(np.float64)


def striped(idx):
    return np.tile(np.asarray(idx).reshape(-1, 16).T, (8, 1)).astype(np.uint16)


def unstriped(offs):
    return offs[:16].T.reshape(-1).astype(np.int64)


def striped8(idx):
    return np.asarray(idx).reshape(8, -1, 16).transpose(0, 2, 1).reshape(128, -1).astype(np.uint16)


def unstriped8(offs):
    return offs.reshape(8, 16, -1).transpose(0, 2, 1).reshape(8, -1).astype(np.int64)


def pick8(x, idx, run):
    r = np.arange(len(x))
    return x[r[:, None], idx[r % (8 * run) // run]]


E2M1 = np.array([0.0, 0.5, 1.0, 1.5, 2.0, 3.0, 4.0, 6.0, -0.0, -0.5, -1.0, -1.5, -2.0, -3.0, -4.0, -6.0])


def pack_weight(w, fmt):
    k, n = w.shape
    w = f64(np.asarray(w, np.float32).astype(ml_dtypes.bfloat16)).reshape(k // 32, 32, n)
    amax = np.abs(w).max(1)
    if fmt == "e4m3":
        byte = np.frexp(amax)[1] - 1 + 127 - 7
    else:
        mant, ex = np.frexp(amax / 6.0)
        byte = np.where(mant > 0.5, ex, ex - 1) + 127
    byte = np.clip(np.where(amax > 0, byte, 1), 1, 254)
    scaled = (w * np.exp2(127.0 - byte)[:, None, :]).reshape(k, n).astype(np.float32)
    by_word = np.ascontiguousarray(scaled.reshape(k // 512, 128, 4, n).transpose(0, 1, 3, 2))
    if fmt == "e4m3":
        words = by_word.astype(ml_dtypes.float8_e4m3fn).view(np.uint8)
    else:
        c = by_word.astype(ml_dtypes.float4_e2m1fn).view(np.uint8) & 0xF
        words = (c[..., 0::2] | (c[..., 1::2] << 4)).reshape(k // 512, 128, 2 * n)
    return np.ascontiguousarray(words), np.ascontiguousarray(byte.astype(np.uint8).reshape(k // 512, 16, n))


def unpack_weight(words, scales, fmt):
    g, _, n = scales.shape
    words = np.ascontiguousarray(words).reshape(g, 128, n, -1)
    if fmt == "e4m3":
        vals = words.view(ml_dtypes.float8_e4m3fn).astype(np.float64)
    else:
        nib = np.empty((g, 128, n, 4), np.uint8)
        nib[..., 0::2] = words & 0xF
        nib[..., 1::2] = words >> 4
        vals = E2M1[nib]
    vals = vals * np.repeat(np.exp2(scales.astype(np.float64) - 127.0), 8, axis=1)[..., None]
    return vals.transpose(0, 1, 3, 2).reshape(g * 512, n)


K, J, R, T, F, O, C, N = 512, 256, 512, 1024, 1024, 128, 512, 256


def setup_inputs():
    n = np.random.standard_normal
    idx = np.random.permutation(T)[:J]
    idx2 = np.stack([np.random.permutation(F)[:R] for _ in range(8)])
    idx3 = np.stack([np.random.permutation(C)[:J] for _ in range(8)])
    idx4 = np.stack([np.random.permutation(C)[:O] for _ in range(8)])
    idx5 = np.stack([np.random.permutation(C)[:O] for _ in range(8)])
    fk = mx_kscale(K)
    fr = mx_kscale(R)
    xtp = pack_weight(n((K, T)) * fk[:, None], "e2m1")
    wbp = pack_weight(n((R, N)) * 1 / np.sqrt(R) / fr[:, None], "e2m1")
    return {
        "xt_words": xtp[0],
        "xt_scales": xtp[1],
        "ua": (np.random.randint(-7, 8, (K, F)).astype(np.float64)).astype(np.float32),
        "ha": ((np.random.randint(8, 25, (K, 1)) / 1024.0) / fk[:, None]).astype(np.float32),
        "sa": (np.random.uniform(0.5, 1.6, (R, 1)) * fr[:, None]).astype(np.float32),
        "sb": (np.random.uniform(0.5, 1.6, (R, 1)) * fr[:, None]).astype(np.float32),
        "wb_words": wbp[0],
        "wb_scales": wbp[1],
        "offs": striped(idx),
        "offs2": striped8(idx2),
        "offs3": striped8(idx3),
        "offs4": striped8(idx4),
        "offs5": striped8(idx5),
    }


def reference(xt_words, xt_scales, ua, ha, sa, sb, wb_words, wb_scales, offs, offs2, offs3, offs4, offs5):
    idx = unstriped(offs)
    idx2 = unstriped8(offs2)
    idx3 = unstriped8(offs3)
    idx4 = unstriped8(offs4)
    idx5 = unstriped8(offs5)
    xtu = unpack_weight(xt_words, xt_scales, "e2m1")
    wbu = unpack_weight(wb_words, wb_scales, "e2m1")
    wc = pick8(f64(ua), idx2, 64) * f64(ha)
    wcq = mxq(wc, 0, "e4m3")
    xtidxg = xtu[:, idx]
    a = wcq.T @ xtidxg
    pw = np.zeros((R, C))
    pw[np.arange(R)[:, None], idx3[np.arange(R) % 512 // 64]] = a
    hid = np.maximum(pick8(pw, idx4, 64) * f64(sa), pick8(pw, idx5, 64) * f64(sb))
    hidq = mxq(hid, 0, "e4m3")
    y = wbu.T @ hidq
    return y

@@ -1,0 +1,199 @@
+from contextlib import ExitStack
+
+import concourse.mybir as mybir
+
+K, J, R, T, F, O, C, N = 512, 256, 512, 1024, 1024, 128, 512, 256
+FLOPS = 2 * K * R * J + 2 * R * N * O
+
+F32 = mybir.dt.float32
+BF16 = mybir.dt.bfloat16
+I32 = mybir.dt.int32
+U32 = mybir.dt.uint32
+U16 = mybir.dt.uint16
+U8 = mybir.dt.uint8
+FP8X4 = mybir.dt.float8_e4m3fn_x4
+FP4X4 = mybir.dt.float4_e2m1fn_x4
+COPY = mybir.ActivationFunctionType.Copy
+MAX = mybir.AluOpType.max
+
+P = 128
+PACK = 4
+HALF = R // 2
+
+
+def tile_picked_tokens_codes_one_boardpair_one_plain_kernel(
+    tc, xt_words, xt_scales, ua, ha, sa, sb, wb_words, wb_scales, offs, offs2, offs3, offs4, offs5, out
+):
+    nc = tc.nc
+    with ExitStack() as ctx:
+        keep = ctx.enter_context(tc.tile_pool(name="keep", bufs=1))
+        psum = ctx.enter_context(tc.psum_pool(name="psum", bufs=1))
+
+        tok_list = keep.tile([P, J // 16], U16, name="tok_list")
+        code_list = keep.tile([P, R // 16], U16, name="code_list")
+        put_list = keep.tile([P, J // 16], U16, name="put_list")
+        first_list = keep.tile([P, O // 16], U16, name="first_list")
+        second_list = keep.tile([P, O // 16], U16, name="second_list")
+
+        table = [keep.tile([P, F], F32, name="table%d" % t) for t in range(PACK)]
+        step = keep.tile([P, PACK], F32, name="step")
+        first_w = keep.tile([P, PACK], F32, name="first_w")
+        second_w = keep.tile([P, PACK], F32, name="second_w")
+        x_words = keep.tile([P, T], U16, name="x_words")
+        x_stage = keep.tile([P, 2 * T], U8, name="x_stage")
+        x_bytes = keep.tile([P, T], U8, name="x_bytes")
+        w_words = keep.tile([P, 2 * N], U8, name="w_words", align_bytes=64)
+        w_bytes = keep.tile([P, N], U8, name="w_bytes", align_bytes=64)
+        board = [keep.tile([P, C], F32, name="board%d" % t) for t in range(PACK)]
+
+        ua_rows = ua.rearrange("(p t) f -> t p f", t=PACK)
+        xs_rows = xt_scales[0].bitcast(I32)
+        ws_rows = wb_scales[0].bitcast(I32)
+        stage32 = x_stage[:].bitcast(I32)
+
+        nc.scalar.dma_start(out=step[:], in_=ha.rearrange("(p t) o -> p (t o)", t=PACK))
+        nc.sync.dma_start(out=table[0][:], in_=ua_rows[0])
+        nc.sync.dma_start(code_list[:], offs2)
+        nc.sync.dma_start(out=table[1][:], in_=ua_rows[1])
+        nc.sync.dma_start(out=table[2][:], in_=ua_rows[2])
+        nc.sync.dma_start(tok_list[:], offs)
+        for h in range(2):
+            nc.sync.dma_start(
+                out=stage32[64 * h : 64 * h + 4, :].rearrange("i (q c) -> i q c", q=2),
+                in_=xs_rows[8 * h : 8 * h + 8, :].rearrange("(q i) c -> i q c", q=2),
+            )
+        nc.sync.dma_start(out=table[3][:], in_=ua_rows[3])
+        nc.sync.dma_start(out=x_words[:].bitcast(I32), in_=xt_words[0].bitcast(I32))
+        nc.sync.dma_start(put_list[:], offs3)
+        nc.sync.dma_start(first_list[:], offs4)
+        nc.sync.dma_start(second_list[:], offs5)
+        nc.gpsimd.dma_start(out=first_w[:], in_=sa.rearrange("(p t) o -> p (t o)", t=PACK))
+        nc.gpsimd.dma_start(out=second_w[:], in_=sb.rearrange("(p t) o -> p (t o)", t=PACK))
+        nc.sync.dma_start(out=w_words[:].bitcast(I32), in_=wb_words[0].bitcast(I32))
+
+        nc.vector.memset(x_bytes[:].bitcast(I32), 0)
+        nc.vector.memset(w_bytes[:].bitcast(I32), 0)
+        for t in range(PACK):
+            nc.vector.memset(board[t][:], 0.0)
+        for q in range(4):
+            nc.sync.dma_start(out=w_bytes[:].bitcast(I32)[32 * q : 32 * q + 4, :], in_=ws_rows[4 * q : 4 * q + 4, :])
+
+        words32 = T // 4
+        for q in range(4):
+            src = 64 * (q // 2)
+            nc.vector.tensor_copy(
+                out=x_bytes[:].bitcast(I32)[32 * q : 32 * q + 4, :],
+                in_=stage32[src : src + 4, (q % 2) * words32 : (q % 2 + 1) * words32],
+            )
+        picked_bytes = keep.tile([P, J], U8, name="picked_bytes", align_bytes=64)
+        picked_words = keep.tile([P, J], U16, name="picked_words", align_bytes=64)
+        nc.vector.tensor_copy(picked_bytes[:], x_bytes[:].indirect(tok_list[:]))
+        nc.vector.tensor_copy(picked_words[:], x_words[:].indirect(tok_list[:]))
+
+        wc = [keep.tile([P, PACK, HALF], BF16, name="wc%d" % h) for h in range(2)]
+        for t in range(PACK):
+            for h in range(2):
+                cols = HALF // 16
+                nc.scalar.activation(
+                    out=wc[h][:, t, :],
+                    in_=table[t][:].indirect(code_list[:, h * cols : (h + 1) * cols]),
+                    func=COPY,
+                    scale=step[:, t : t + 1],
+                )
+
+        woven = [keep.tile([P, P, PACK], BF16, name="woven%d" % u, align_bytes=64) for u in range(PACK)]
+        wc_codes = [keep.tile([P, P], U32, name="wc_codes%d" % u, align_bytes=64) for u in range(PACK)]
+        wc_bytes = [keep.tile([P, P], U8, name="wc_bytes%d" % u, align_bytes=64) for u in range(PACK)]
+        pieces = [(u, 0, J) for u in range(PACK)]
+        a_bank = [psum.tile([P, hi - lo], F32, name="a_bank%d" % i) for i, (u, lo, hi) in enumerate(pieces)]
+        a_rows = [keep.tile([P, hi - lo], F32, name="a_rows%d" % i) for i, (u, lo, hi) in enumerate(pieces)]
+
+        def weave(copy, h, u):
+            copy(
+                out=woven[u][:, 64 * h : 64 * h + 64, :],
+                in_=wc[h][:].rearrange("p t (m u) -> p u m t", u=PACK)[:, u, :, :],
+            )
+
+        def quantise(u):
+            nc.vector.quantize_mx(
+                out=wc_codes[u][:].bitcast(FP8X4),
+                scales=wc_bytes[u][:],
+                in_=woven[u][:].rearrange("p m t -> p (m t)"),
+            )
+
+        def product(i):
+            u, lo, hi = pieces[i]
+            nc.tensor.matmul_mx(
+                out=a_bank[i][:],
+                lhsT=wc_codes[u][:].bitcast(FP8X4),
+                lhsT_scale=wc_bytes[u][:],
+                rhs=picked_words[:, lo:hi].bitcast(FP4X4),
+                rhs_scale=picked_bytes[:, lo:hi],
+                start=True,
+                stop=True,
+            )
+            nc.scalar.copy(out=a_rows[i][:], in_=a_bank[i][:])
+
+        def scatter(i):
+            u, lo, hi = pieces[i]
+            nc.vector.tensor_copy(board[u][:].indirect(put_list[:, lo // 16 : hi // 16]), a_rows[i][:])
+
+        weave(nc.vector.tensor_copy, 0, 0)
+        weave(nc.vector.tensor_copy, 1, 0)
+        weave(nc.vector.tensor_copy, 0, 1)
+        for u in range(1, PACK):
+            weave(nc.scalar.copy, 1, u)
+        weave(nc.scalar.copy, 0, 3)
+        quantise(0)
+        weave(nc.vector.tensor_copy, 0, 2)
+        quantise(1)
+        quantise(2)
+        quantise(3)
+        for i in range(PACK):
+            product(i)
+        for i in range(PACK):
+            scatter(i)
+
+        early = PACK - 1
+        first_early = keep.tile([P, early, O], F32, name="first_early")
+        second_early = keep.tile([P, early, O], F32, name="second_early")
+        first_last = keep.tile([P, O], F32, name="first_last")
+        second_last = keep.tile([P, O], F32, name="second_last")
+        for u in range(PACK):
+            dst1 = first_early[:, u, :] if u < early else first_last[:]
+            dst2 = second_early[:, u, :] if u < early else second_last[:]
+            nc.scalar.activation(out=dst1, in_=board[u][:].indirect(first_list[:]), func=COPY, scale=first_w[:, u : u + 1])
+            nc.scalar.activation(out=dst2, in_=board[u][:].indirect(second_list[:]), func=COPY, scale=second_w[:, u : u + 1])
+
+        hid = keep.tile([P, O, PACK], BF16, name="hid", align_bytes=64)
+        nc.vector.tensor_tensor(
+            out=hid[:, :, 0:early],
+            in0=first_early[:].rearrange("p u o -> p o u"),
+            in1=second_early[:].rearrange("p u o -> p o u"),
+            op=MAX,
+        )
+        nc.vector.tensor_tensor(out=hid[:, :, early], in0=first_last[:], in1=second_last[:], op=MAX)
+        hid_codes = keep.tile([P, O], U32, name="hid_codes", align_bytes=64)
+        hid_bytes = keep.tile([P, O], U8, name="hid_bytes", align_bytes=64)
+        nc.vector.quantize_mx(
+            out=hid_codes[:].bitcast(FP8X4), scales=hid_bytes[:], in_=hid[:].rearrange("p o u -> p (o u)")
+        )
+
+        for g in range(N // P):
+            y_bank = psum.tile([P, O], F32, name="y_bank%d" % g)
+            y_rows = keep.tile([P, O], F32, name="y_rows%d" % g)
+            nc.tensor.matmul_mx(
+                out=y_bank[:],
+                lhsT=w_words[:, 2 * P * g : 2 * P * (g + 1)].bitcast(FP4X4),
+                lhsT_scale=w_bytes[:, P * g : P * (g + 1)],
+                rhs=hid_codes[:].bitcast(FP8X4),
+                rhs_scale=hid_bytes[:],
+                start=True,
+                stop=True,
+            )
+            if g == 0:
+                nc.scalar.copy(out=y_rows[:], in_=y_bank[:])
+                nc.scalar.dma_start(out=out[P * g : P * (g + 1), :], in_=y_rows[:])
+            else:
+                nc.vector.tensor_copy(out=y_rows[:], in_=y_bank[:])
+                nc.sync.dma_start(out=out[P * g : P * (g + 1), :], in_=y_rows[:])

@@ -46,6 +46,11 @@ def tile_picked_tokens_codes_one_boardpair_one_plain_kernel(
         w_bytes = keep.tile([P, N], U8, name="w_bytes", align_bytes=64)
         board = [keep.tile([P, C], F32, name="board%d" % t) for t in range(PACK)]
 
+        warm_in = keep.tile([P, 1], F32, name="warm_in")
+        warm_out = keep.tile([P, 1], F32, name="warm_out")
+        nc.gpsimd.memset(warm_in[:], 0.0)
+        nc.scalar.activation(out=warm_out[:], in_=warm_in[:], func=COPY)
+
         ua_rows = ua.rearrange("(p t) f -> t p f", t=PACK)
         xs_rows = xt_scales[0].bitcast(I32)
         ws_rows = wb_scales[0].bitcast(I32)

@@ -40,7 +40,6 @@ def tile_picked_tokens_codes_one_boardpair_one_plain_kernel(
         first_w = keep.tile([P, PACK], F32, name="first_w")
         second_w = keep.tile([P, PACK], F32, name="second_w")
         x_words = keep.tile([P, T], U16, name="x_words")
-        x_stage = keep.tile([P, 2 * T], U8, name="x_stage")
         x_bytes = keep.tile([P, T], U8, name="x_bytes")
         w_words = keep.tile([P, 2 * N], U8, name="w_words", align_bytes=64)
         w_bytes = keep.tile([P, N], U8, name="w_bytes", align_bytes=64)
@@ -54,7 +53,7 @@ def tile_picked_tokens_codes_one_boardpair_one_plain_kernel(
         ua_rows = ua.rearrange("(p t) f -> t p f", t=PACK)
         xs_rows = xt_scales[0].bitcast(I32)
         ws_rows = wb_scales[0].bitcast(I32)
-        stage32 = x_stage[:].bitcast(I32)
+        nc.vector.memset(x_bytes[:].bitcast(I32), 0)
 
         nc.scalar.dma_start(out=step[:], in_=ha.rearrange("(p t) o -> p (t o)", t=PACK))
         nc.sync.dma_start(out=table[0][:], in_=ua_rows[0])
@@ -62,11 +61,8 @@ def tile_picked_tokens_codes_one_boardpair_one_plain_kernel(
         nc.sync.dma_start(out=table[1][:], in_=ua_rows[1])
         nc.sync.dma_start(out=table[2][:], in_=ua_rows[2])
         nc.sync.dma_start(tok_list[:], offs)
-        for h in range(2):
-            nc.sync.dma_start(
-                out=stage32[64 * h : 64 * h + 4, :].rearrange("i (q c) -> i q c", q=2),
-                in_=xs_rows[8 * h : 8 * h + 8, :].rearrange("(q i) c -> i q c", q=2),
-            )
+        for i in range(4):
+            nc.sync.dma_start(out=x_bytes[:].bitcast(I32)[i:P:32, :], in_=xs_rows[i:16:4, :])
         nc.sync.dma_start(out=table[3][:], in_=ua_rows[3])
         nc.sync.dma_start(out=x_words[:].bitcast(I32), in_=xt_words[0].bitcast(I32))
         nc.sync.dma_start(put_list[:], offs3)
@@ -76,20 +72,12 @@ def tile_picked_tokens_codes_one_boardpair_one_plain_kernel(
         nc.gpsimd.dma_start(out=second_w[:], in_=sb.rearrange("(p t) o -> p (t o)", t=PACK))
         nc.sync.dma_start(out=w_words[:].bitcast(I32), in_=wb_words[0].bitcast(I32))
 
-        nc.vector.memset(x_bytes[:].bitcast(I32), 0)
         nc.vector.memset(w_bytes[:].bitcast(I32), 0)
         for t in range(PACK):
             nc.vector.memset(board[t][:], 0.0)
         for q in range(4):
             nc.sync.dma_start(out=w_bytes[:].bitcast(I32)[32 * q : 32 * q + 4, :], in_=ws_rows[4 * q : 4 * q + 4, :])
 
-        words32 = T // 4
-        for q in range(4):
-            src = 64 * (q // 2)
-            nc.vector.tensor_copy(
-                out=x_bytes[:].bitcast(I32)[32 * q : 32 * q + 4, :],
-                in_=stage32[src : src + 4, (q % 2) * words32 : (q % 2 + 1) * words32],
-            )
         picked_bytes = keep.tile([P, J], U8, name="picked_bytes", align_bytes=64)
         picked_words = keep.tile([P, J], U16, name="picked_words", align_bytes=64)
         nc.vector.tensor_copy(picked_bytes[:], x_bytes[:].indirect(tok_list[:]))
@@ -106,24 +94,32 @@ def tile_picked_tokens_codes_one_boardpair_one_plain_kernel(
                     scale=step[:, t : t + 1],
                 )
 
-        woven = [keep.tile([P, P, PACK], BF16, name="woven%d" % u, align_bytes=64) for u in range(PACK)]
+        woven_first = keep.tile([P, P, PACK], BF16, name="woven_first", align_bytes=64)
+        woven_rest = keep.tile([P, PACK - 1, P, PACK], BF16, name="woven_rest", align_bytes=64)
+        woven = [woven_first[:]] + [woven_rest[:, u, :, :] for u in range(PACK - 1)]
         wc_codes = [keep.tile([P, P], U32, name="wc_codes%d" % u, align_bytes=64) for u in range(PACK)]
         wc_bytes = [keep.tile([P, P], U8, name="wc_bytes%d" % u, align_bytes=64) for u in range(PACK)]
         pieces = [(u, 0, J) for u in range(PACK)]
         a_bank = [psum.tile([P, hi - lo], F32, name="a_bank%d" % i) for i, (u, lo, hi) in enumerate(pieces)]
         a_rows = [keep.tile([P, hi - lo], F32, name="a_rows%d" % i) for i, (u, lo, hi) in enumerate(pieces)]
 
-        def weave(copy, h, u):
+        def weave_first(h):
+            nc.vector.tensor_copy(
+                out=woven_first[:, 64 * h : 64 * h + 64, :],
+                in_=wc[h][:].rearrange("p t (m u) -> p u m t", u=PACK)[:, 0, :, :],
+            )
+
+        def weave_rest(copy, h):
             copy(
-                out=woven[u][:, 64 * h : 64 * h + 64, :],
-                in_=wc[h][:].rearrange("p t (m u) -> p u m t", u=PACK)[:, u, :, :],
+                out=woven_rest[:, :, 64 * h : 64 * h + 64, :].rearrange("p u m t -> p m t u"),
+                in_=wc[h][:].rearrange("p t (m u) -> p m t u", u=PACK)[:, :, :, 1:PACK],
             )
 
         def quantise(u):
             nc.vector.quantize_mx(
                 out=wc_codes[u][:].bitcast(FP8X4),
                 scales=wc_bytes[u][:],
-                in_=woven[u][:].rearrange("p m t -> p (m t)"),
+                in_=woven[u].rearrange("p m t -> p (m t)"),
             )
 
         def product(i):
@@ -143,17 +139,12 @@ def tile_picked_tokens_codes_one_boardpair_one_plain_kernel(
             u, lo, hi = pieces[i]
             nc.vector.tensor_copy(board[u][:].indirect(put_list[:, lo // 16 : hi // 16]), a_rows[i][:])
 
-        weave(nc.vector.tensor_copy, 0, 0)
-        weave(nc.vector.tensor_copy, 1, 0)
-        weave(nc.vector.tensor_copy, 0, 1)
-        for u in range(1, PACK):
-            weave(nc.scalar.copy, 1, u)
-        weave(nc.scalar.copy, 0, 3)
-        quantise(0)
-        weave(nc.vector.tensor_copy, 0, 2)
-        quantise(1)
-        quantise(2)
-        quantise(3)
+        weave_first(0)
+        weave_first(1)
+        weave_rest(nc.scalar.copy, 1)
+        weave_rest(nc.vector.tensor_copy, 0)
+        for u in range(PACK):
+            quantise(u)
         for i in range(PACK):
             product(i)
         for i in range(PACK):

@@ -94,32 +94,30 @@ def tile_picked_tokens_codes_one_boardpair_one_plain_kernel(
                     scale=step[:, t : t + 1],
                 )
 
-        woven_first = keep.tile([P, P, PACK], BF16, name="woven_first", align_bytes=64)
-        woven_rest = keep.tile([P, PACK - 1, P, PACK], BF16, name="woven_rest", align_bytes=64)
-        woven = [woven_first[:]] + [woven_rest[:, u, :, :] for u in range(PACK - 1)]
+        M = P // 2
+        first_lo = keep.tile([P, M, PACK], BF16, name="first_lo", align_bytes=64)
+        first_hi = keep.tile([P, M, PACK], BF16, name="first_hi", tag="reused", align_bytes=64)
+        rest_hi = keep.tile([P, PACK - 1, M, PACK], BF16, name="rest_hi", align_bytes=64)
         wc_codes = [keep.tile([P, P], U32, name="wc_codes%d" % u, align_bytes=64) for u in range(PACK)]
         wc_bytes = [keep.tile([P, P], U8, name="wc_bytes%d" % u, align_bytes=64) for u in range(PACK)]
         pieces = [(u, 0, J) for u in range(PACK)]
         a_bank = [psum.tile([P, hi - lo], F32, name="a_bank%d" % i) for i, (u, lo, hi) in enumerate(pieces)]
         a_rows = [keep.tile([P, hi - lo], F32, name="a_rows%d" % i) for i, (u, lo, hi) in enumerate(pieces)]
 
-        def weave_first(h):
-            nc.vector.tensor_copy(
-                out=woven_first[:, 64 * h : 64 * h + 64, :],
-                in_=wc[h][:].rearrange("p t (m u) -> p u m t", u=PACK)[:, 0, :, :],
-            )
+        def weave_first(dst, h):
+            nc.vector.tensor_copy(out=dst[:], in_=wc[h][:].rearrange("p t (m u) -> p u m t", u=PACK)[:, 0, :, :])
 
-        def weave_rest(copy, h):
+        def weave_rest(copy, dst, h):
             copy(
-                out=woven_rest[:, :, 64 * h : 64 * h + 64, :].rearrange("p u m t -> p m t u"),
+                out=dst[:].rearrange("p u m t -> p m t u"),
                 in_=wc[h][:].rearrange("p t (m u) -> p m t u", u=PACK)[:, :, :, 1:PACK],
             )
 
-        def quantise(u):
+        def quantise(src, u, h):
             nc.vector.quantize_mx(
-                out=wc_codes[u][:].bitcast(FP8X4),
-                scales=wc_bytes[u][:],
-                in_=woven[u].rearrange("p m t -> p (m t)"),
+                out=wc_codes[u][:, M * h : M * (h + 1)].bitcast(FP8X4),
+                scales=wc_bytes[u][:, M * h : M * (h + 1)],
+                in_=src.rearrange("p m t -> p (m t)"),
             )
 
         def product(i):
@@ -139,12 +137,17 @@ def tile_picked_tokens_codes_one_boardpair_one_plain_kernel(
             u, lo, hi = pieces[i]
             nc.vector.tensor_copy(board[u][:].indirect(put_list[:, lo // 16 : hi // 16]), a_rows[i][:])
 
-        weave_first(0)
-        weave_first(1)
-        weave_rest(nc.scalar.copy, 1)
-        weave_rest(nc.vector.tensor_copy, 0)
-        for u in range(PACK):
-            quantise(u)
+        weave_first(first_lo, 0)
+        weave_first(first_hi, 1)
+        weave_rest(nc.scalar.copy, rest_hi, 1)
+        quantise(first_lo[:], 0, 0)
+        quantise(first_hi[:], 0, 1)
+        rest_lo = keep.tile([P, PACK - 1, M, PACK], BF16, name="rest_lo", tag="reused", align_bytes=64)
+        weave_rest(nc.vector.tensor_copy, rest_lo, 0)
+        for u in range(1, PACK):
+            quantise(rest_hi[:, u - 1, :, :], u, 1)
+        for u in range(1, PACK):
+            quantise(rest_lo[:, u - 1, :, :], u, 0)
         for i in range(PACK):
             product(i)
         for i in range(PACK):

@@ -153,25 +153,30 @@ def tile_picked_tokens_codes_one_boardpair_one_plain_kernel(
         for i in range(PACK):
             scatter(i)
 
-        early = PACK - 1
-        first_early = keep.tile([P, early, O], F32, name="first_early")
-        second_early = keep.tile([P, early, O], F32, name="second_early")
-        first_last = keep.tile([P, O], F32, name="first_last")
-        second_last = keep.tile([P, O], F32, name="second_last")
+        first_read = [keep.tile([P, 2, O], F32, name="first_read%d" % v) for v in range(2)]
+        second_read = [keep.tile([P, 2, O], F32, name="second_read%d" % v) for v in range(2)]
         for u in range(PACK):
-            dst1 = first_early[:, u, :] if u < early else first_last[:]
-            dst2 = second_early[:, u, :] if u < early else second_last[:]
-            nc.scalar.activation(out=dst1, in_=board[u][:].indirect(first_list[:]), func=COPY, scale=first_w[:, u : u + 1])
-            nc.scalar.activation(out=dst2, in_=board[u][:].indirect(second_list[:]), func=COPY, scale=second_w[:, u : u + 1])
+            nc.scalar.activation(
+                out=first_read[u // 2][:, u % 2, :],
+                in_=board[u][:].indirect(first_list[:]),
+                func=COPY,
+                scale=first_w[:, u : u + 1],
+            )
+            nc.scalar.activation(
+                out=second_read[u // 2][:, u % 2, :],
+                in_=board[u][:].indirect(second_list[:]),
+                func=COPY,
+                scale=second_w[:, u : u + 1],
+            )
 
         hid = keep.tile([P, O, PACK], BF16, name="hid", align_bytes=64)
-        nc.vector.tensor_tensor(
-            out=hid[:, :, 0:early],
-            in0=first_early[:].rearrange("p u o -> p o u"),
-            in1=second_early[:].rearrange("p u o -> p o u"),
-            op=MAX,
-        )
-        nc.vector.tensor_tensor(out=hid[:, :, early], in0=first_last[:], in1=second_last[:], op=MAX)
+        for v in range(2):
+            nc.vector.tensor_tensor(
+                out=hid[:, :, 2 * v : 2 * v + 2],
+                in0=first_read[v][:].rearrange("p u o -> p o u"),
+                in1=second_read[v][:].rearrange("p u o -> p o u"),
+                op=MAX,
+            )
         hid_codes = keep.tile([P, O], U32, name="hid_codes", align_bytes=64)
         hid_bytes = keep.tile([P, O], U8, name="hid_bytes", align_bytes=64)
         nc.vector.quantize_mx(

from contextlib import ExitStack

import concourse.mybir as mybir

K, J, R, T, F, O, C, N = 512, 256, 512, 1024, 1024, 128, 512, 256
FLOPS = 2 * K * R * J + 2 * R * N * O

F32 = mybir.dt.float32
BF16 = mybir.dt.bfloat16
I32 = mybir.dt.int32
U32 = mybir.dt.uint32
U16 = mybir.dt.uint16
U8 = mybir.dt.uint8
FP8X4 = mybir.dt.float8_e4m3fn_x4
FP4X4 = mybir.dt.float4_e2m1fn_x4
COPY = mybir.ActivationFunctionType.Copy
MAX = mybir.AluOpType.max

P = 128
PACK = 4
HALF = R // 2


def tile_picked_tokens_codes_one_boardpair_one_plain_kernel(
    tc, xt_words, xt_scales, ua, ha, sa, sb, wb_words, wb_scales, offs, offs2, offs3, offs4, offs5, out
):
    nc = tc.nc
    with ExitStack() as ctx:
        keep = ctx.enter_context(tc.tile_pool(name="keep", bufs=1))
        psum = ctx.enter_context(tc.psum_pool(name="psum", bufs=1))

        tok_list = keep.tile([P, J // 16], U16, name="tok_list")
        code_list = keep.tile([P, R // 16], U16, name="code_list")
        put_list = keep.tile([P, J // 16], U16, name="put_list")
        first_list = keep.tile([P, O // 16], U16, name="first_list")
        second_list = keep.tile([P, O // 16], U16, name="second_list")

        table = [keep.tile([P, F], F32, name="table%d" % t) for t in range(PACK)]
        step = keep.tile([P, PACK], F32, name="step")
        first_w = keep.tile([P, PACK], F32, name="first_w")
        second_w = keep.tile([P, PACK], F32, name="second_w")
        x_words = keep.tile([P, T], U16, name="x_words")
        x_bytes = keep.tile([P, T], U8, name="x_bytes")
        w_words = keep.tile([P, 2 * N], U8, name="w_words", align_bytes=64)
        w_bytes = keep.tile([P, N], U8, name="w_bytes", align_bytes=64)
        board = [keep.tile([P, C], F32, name="board%d" % t) for t in range(PACK)]

        warm_in = keep.tile([P, 1], F32, name="warm_in")
        warm_out = keep.tile([P, 1], F32, name="warm_out")
        nc.gpsimd.memset(warm_in[:], 0.0)
        nc.scalar.activation(out=warm_out[:], in_=warm_in[:], func=COPY)

        ua_rows = ua.rearrange("(p t) f -> t p f", t=PACK)
        xs_rows = xt_scales[0].bitcast(I32)
        ws_rows = wb_scales[0].bitcast(I32)
        nc.vector.memset(x_bytes[:].bitcast(I32), 0)

        nc.scalar.dma_start(out=step[:], in_=ha.rearrange("(p t) o -> p (t o)", t=PACK))
        nc.sync.dma_start(out=table[0][:], in_=ua_rows[0])
        nc.sync.dma_start(code_list[:], offs2)
        nc.sync.dma_start(out=table[1][:], in_=ua_rows[1])
        nc.sync.dma_start(out=table[2][:], in_=ua_rows[2])
        nc.sync.dma_start(tok_list[:], offs)
        for i in range(4):
            nc.sync.dma_start(out=x_bytes[:].bitcast(I32)[i:P:32, :], in_=xs_rows[i:16:4, :])
        nc.sync.dma_start(out=table[3][:], in_=ua_rows[3])
        nc.sync.dma_start(out=x_words[:].bitcast(I32), in_=xt_words[0].bitcast(I32))
        nc.sync.dma_start(put_list[:], offs3)
        nc.sync.dma_start(first_list[:], offs4)
        nc.sync.dma_start(second_list[:], offs5)
        nc.gpsimd.dma_start(out=first_w[:], in_=sa.rearrange("(p t) o -> p (t o)", t=PACK))
        nc.gpsimd.dma_start(out=second_w[:], in_=sb.rearrange("(p t) o -> p (t o)", t=PACK))
        nc.sync.dma_start(out=w_words[:].bitcast(I32), in_=wb_words[0].bitcast(I32))

        nc.vector.memset(w_bytes[:].bitcast(I32), 0)
        for t in range(PACK):
            nc.vector.memset(board[t][:], 0.0)
        for q in range(4):
            nc.sync.dma_start(out=w_bytes[:].bitcast(I32)[32 * q : 32 * q + 4, :], in_=ws_rows[4 * q : 4 * q + 4, :])

        picked_bytes = keep.tile([P, J], U8, name="picked_bytes", align_bytes=64)
        picked_words = keep.tile([P, J], U16, name="picked_words", align_bytes=64)
        nc.vector.tensor_copy(picked_bytes[:], x_bytes[:].indirect(tok_list[:]))
        nc.vector.tensor_copy(picked_words[:], x_words[:].indirect(tok_list[:]))

        wc = [keep.tile([P, PACK, HALF], BF16, name="wc%d" % h) for h in range(2)]
        for t in range(PACK):
            for h in range(2):
                cols = HALF // 16
                nc.scalar.activation(
                    out=wc[h][:, t, :],
                    in_=table[t][:].indirect(code_list[:, h * cols : (h + 1) * cols]),
                    func=COPY,
                    scale=step[:, t : t + 1],
                )

        M = P // 2
        first_lo = keep.tile([P, M, PACK], BF16, name="first_lo", align_bytes=64)
        first_hi = keep.tile([P, M, PACK], BF16, name="first_hi", tag="reused", align_bytes=64)
        rest_hi = keep.tile([P, PACK - 1, M, PACK], BF16, name="rest_hi", align_bytes=64)
        wc_codes = [keep.tile([P, P], U32, name="wc_codes%d" % u, align_bytes=64) for u in range(PACK)]
        wc_bytes = [keep.tile([P, P], U8, name="wc_bytes%d" % u, align_bytes=64) for u in range(PACK)]
        pieces = [(u, 0, J) for u in range(PACK)]
        a_bank = [psum.tile([P, hi - lo], F32, name="a_bank%d" % i) for i, (u, lo, hi) in enumerate(pieces)]
        a_rows = [keep.tile([P, hi - lo], F32, name="a_rows%d" % i) for i, (u, lo, hi) in enumerate(pieces)]

        def weave_first(dst, h):
            nc.vector.tensor_copy(out=dst[:], in_=wc[h][:].rearrange("p t (m u) -> p u m t", u=PACK)[:, 0, :, :])

        def weave_rest(copy, dst, h):
            copy(
                out=dst[:].rearrange("p u m t -> p m t u"),
                in_=wc[h][:].rearrange("p t (m u) -> p m t u", u=PACK)[:, :, :, 1:PACK],
            )

        def quantise(src, u, h):
            nc.vector.quantize_mx(
                out=wc_codes[u][:, M * h : M * (h + 1)].bitcast(FP8X4),
                scales=wc_bytes[u][:, M * h : M * (h + 1)],
                in_=src.rearrange("p m t -> p (m t)"),
            )

        def product(i):
            u, lo, hi = pieces[i]
            nc.tensor.matmul_mx(
                out=a_bank[i][:],
                lhsT=wc_codes[u][:].bitcast(FP8X4),
                lhsT_scale=wc_bytes[u][:],
                rhs=picked_words[:, lo:hi].bitcast(FP4X4),
                rhs_scale=picked_bytes[:, lo:hi],
                start=True,
                stop=True,
            )
            nc.scalar.copy(out=a_rows[i][:], in_=a_bank[i][:])

        def scatter(i):
            u, lo, hi = pieces[i]
            nc.vector.tensor_copy(board[u][:].indirect(put_list[:, lo // 16 : hi // 16]), a_rows[i][:])

        weave_first(first_lo, 0)
        weave_first(first_hi, 1)
        weave_rest(nc.scalar.copy, rest_hi, 1)
        quantise(first_lo[:], 0, 0)
        quantise(first_hi[:], 0, 1)
        rest_lo = keep.tile([P, PACK - 1, M, PACK], BF16, name="rest_lo", tag="reused", align_bytes=64)
        weave_rest(nc.vector.tensor_copy, rest_lo, 0)
        for u in range(1, PACK):
            quantise(rest_hi[:, u - 1, :, :], u, 1)
        for u in range(1, PACK):
            quantise(rest_lo[:, u - 1, :, :], u, 0)
        for i in range(PACK):
            product(i)
        for i in range(PACK):
            scatter(i)

        first_read = [keep.tile([P, 2, O], F32, name="first_read%d" % v) for v in range(2)]
        second_read = [keep.tile([P, 2, O], F32, name="second_read%d" % v) for v in range(2)]
        for u in range(PACK):
            nc.scalar.activation(
                out=first_read[u // 2][:, u % 2, :],
                in_=board[u][:].indirect(first_list[:]),
                func=COPY,
                scale=first_w[:, u : u + 1],
            )
            nc.scalar.activation(
                out=second_read[u // 2][:, u % 2, :],
                in_=board[u][:].indirect(second_list[:]),
                func=COPY,
                scale=second_w[:, u : u + 1],
            )

        hid = keep.tile([P, O, PACK], BF16, name="hid", align_bytes=64)
        for v in range(2):
            nc.vector.tensor_tensor(
                out=hid[:, :, 2 * v : 2 * v + 2],
                in0=first_read[v][:].rearrange("p u o -> p o u"),
                in1=second_read[v][:].rearrange("p u o -> p o u"),
                op=MAX,
            )
        hid_codes = keep.tile([P, O], U32, name="hid_codes", align_bytes=64)
        hid_bytes = keep.tile([P, O], U8, name="hid_bytes", align_bytes=64)
        nc.vector.quantize_mx(
            out=hid_codes[:].bitcast(FP8X4), scales=hid_bytes[:], in_=hid[:].rearrange("p o u -> p (o u)")
        )

        for g in range(N // P):
            y_bank = psum.tile([P, O], F32, name="y_bank%d" % g)
            y_rows = keep.tile([P, O], F32, name="y_rows%d" % g)
            nc.tensor.matmul_mx(
                out=y_bank[:],
                lhsT=w_words[:, 2 * P * g : 2 * P * (g + 1)].bitcast(FP4X4),
                lhsT_scale=w_bytes[:, P * g : P * (g + 1)],
                rhs=hid_codes[:].bitcast(FP8X4),
                rhs_scale=hid_bytes[:],
                start=True,
                stop=True,
            )
            if g == 0:
                nc.scalar.copy(out=y_rows[:], in_=y_bank[:])
                nc.scalar.dma_start(out=out[P * g : P * (g + 1), :], in_=y_rows[:])
            else:
                nc.vector.tensor_copy(out=y_rows[:], in_=y_bank[:])
                nc.sync.dma_start(out=out[P * g : P * (g + 1), :], in_=y_rows[:])
